import numpy as np
import ml_dtypes


def mxq(x, axis, fmt="e4m3"):
    dtype, down = {"e4m3": (ml_dtypes.float8_e4m3fn, 7), "e5m2": (ml_dtypes.float8_e5m2, 14)}[fmt]
    v = np.moveaxis(np.asarray(x, np.float32).astype(ml_dtypes.bfloat16).astype(np.float64), axis, -1)
    blocks = v.reshape(v.shape[:-1] + (-1, 32))
    amax = np.abs(blocks).max(-1, keepdims=True)
    byte = np.maximum(np.where(amax > 0, np.frexp(amax)[1] - 1 + 127, 0) - down, 1)
    scale = np.exp2(byte - 127.0)
    codes = (blocks / scale).astype(np.float32).astype(dtype).astype(np.float64)
    return np.moveaxis((codes * scale).reshape(v.shape), -1, axis)


WIDE = False


def mx_kscale(k):
    if not WIDE:
        return np.ones(k)
    levels = np.array([30, -30])
    if k % 512:
        return np.exp2(np.random.permutation(np.resize(levels, k // 32))).repeat(32)
    a = np.empty((k // 512, 16))
    for p in range(k // 512):
        a[p, :8] = np.random.permutation(np.resize(levels, 8))
        for g in range(8):
            far = levels[np.abs(levels - a[p, g]) >= 10]
            a[p, g + 8] = far[np.random.randint(len(far))]
    return np.exp2(a.ravel()).repeat(32)


def f64(x):
    return np.asarray(x).astype(np.float64)


def striped(idx):
    return np.tile(np.asarray(idx).reshape(-1, 16).T, (8, 1)).astype(np.uint16)


def unstriped(offs):
    return offs[:16].T.reshape(-1).astype(np.int64)


E2M1 = np.array([0.0, 0.5, 1.0, 1.5, 2.0, 3.0, 4.0, 6.0, -0.0, -0.5, -1.0, -1.5, -2.0, -3.0, -4.0, -6.0])


def pack_weight(w, fmt):
    k, n = w.shape
    w = f64(np.asarray(w, np.float32).astype(ml_dtypes.bfloat16)).reshape(k // 32, 32, n)
    amax = np.abs(w).max(1)
    if fmt in ("e4m3", "e5m2"):
        byte = np.frexp(amax)[1] - 1 + 127 - (7 if fmt == "e4m3" else 14)
    else:
        mant, ex = np.frexp(amax / 6.0)
        byte = np.where(mant > 0.5, ex, ex - 1) + 127
    byte = np.clip(np.where(amax > 0, byte, 1), 1, 254)
    scaled = (w * np.exp2(127.0 - byte)[:, None, :]).reshape(k, n).astype(np.float32)
    by_word = np.ascontiguousarray(scaled.reshape(k // 512, 128, 4, n).transpose(0, 1, 3, 2))
    if fmt in ("e4m3", "e5m2"):
        words = by_word.astype(ml_dtypes.float8_e4m3fn if fmt == "e4m3" else ml_dtypes.float8_e5m2).view(np.uint8)
    else:
        c = by_word.astype(ml_dtypes.float4_e2m1fn).view(np.uint8) & 0xF
        words = (c[..., 0::2] | (c[..., 1::2] << 4)).reshape(k // 512, 128, 2 * n)
    return np.ascontiguousarray(words), np.ascontiguousarray(byte.astype(np.uint8).reshape(k // 512, 16, n))


def unpack_weight(words, scales, fmt):
    g, _, n = scales.shape
    words = np.ascontiguousarray(words).reshape(g, 128, n, -1)
    if fmt in ("e4m3", "e5m2"):
        vals = words.view(ml_dtypes.float8_e4m3fn if fmt == "e4m3" else ml_dtypes.float8_e5m2).astype(np.float64)
    else:
        nib = np.empty((g, 128, n, 4), np.uint8)
        nib[..., 0::2] = words & 0xF
        nib[..., 1::2] = words >> 4
        vals = E2M1[nib]
    vals = vals * np.repeat(np.exp2(scales.astype(np.float64) - 127.0), 8, axis=1)[..., None]
    return vals.transpose(0, 1, 3, 2).reshape(g * 512, n)


K, T, J, R, F, V, N = 512, 512, 256, 512, 512, 512, 256


def setup_inputs():
    n = np.random.standard_normal
    idx = np.random.permutation(T)[:J]
    idx2 = np.random.permutation(T)[:J]
    idx3 = np.random.permutation(V)[:J]
    fk = mx_kscale(K)
    fr = mx_kscale(R)
    ff = mx_kscale(F)
    wp = pack_weight(n((K, R)) * 1 / np.sqrt(K) * fk[:, None] * fr, "e4m3")
    w2p = pack_weight(n((F, R)) * 1 / np.sqrt(F) * ff[:, None] * fr, "e5m2")
    wbp = pack_weight(n((R, N)) * 1 / np.sqrt(R) / fr[:, None], "e2m1")
    return {
        "xf": (n((K, T))).astype(np.float32),
        "fk": (np.random.uniform(0.5, 2.0, (K, 1)) / fk[:, None]).astype(np.float32),
        "w_words": wp[0],
        "w_scales": wp[1],
        "so": (n((F, J))).astype(np.float32),
        "fl": (np.random.uniform(0.5, 2.0, (F, 1)) / ff[:, None]).astype(np.float32),
        "w2_words": w2p[0],
        "w2_scales": w2p[1],
        "tb": (n((R, V)) * 0.7 * fr[:, None]).astype(np.float32),
        "wb_words": wbp[0],
        "wb_scales": wbp[1],
        "rs": (1.0 * n((J, N))).astype(np.float32),
        "offs": striped(idx),
        "offs2": striped(idx2),
        "offs3": striped(idx3),
    }


def reference(xf, fk, w_words, w_scales, so, fl, w2_words, w2_scales, tb, wb_words, wb_scales, rs, offs, offs2, offs3):
    idx = unstriped(offs)
    idx2 = unstriped(offs2)
    idx3 = unstriped(offs3)
    wu = unpack_weight(w_words, w_scales, "e4m3")
    w2u = unpack_weight(w2_words, w2_scales, "e5m2")
    wbu = unpack_weight(wb_words, wb_scales, "e2m1")
    u = (f64(xf)[:, idx] - f64(xf)[:, idx2]) * f64(fk)
    s1 = np.pad(f64(so), ((0, 0), (1, 0)))[:, :J]
    u2 = (f64(so) - 0.8 * s1) * f64(fl)
    uq = mxq(u, 0, "e4m3")
    u2q = mxq(u2, 0, "e4m3")
    a = wu.T @ uq + w2u.T @ u2q
    hid = np.maximum(a - f64(tb)[:, idx3], 0.0)
    hidq = mxq(hid, 0, "e5m2")
    p = hidq.T @ wbu
    pk2 = np.max(np.abs(p), axis=1, keepdims=True)
    y = p / (pk2 + 0.2) + 0.3 * f64(rs)
    return y

@@ -1,0 +1,210 @@
+from contextlib import ExitStack
+
+import concourse.mybir as mybir
+
+K, T, J, R, F, V, N = 512, 512, 256, 512, 512, 512, 256
+FLOPS = 2 * J * (K * R + F * R + R * N)
+
+F32 = mybir.dt.float32
+BF16 = mybir.dt.bfloat16
+I32 = mybir.dt.int32
+U32 = mybir.dt.uint32
+U16 = mybir.dt.uint16
+U8 = mybir.dt.uint8
+E4 = mybir.dt.float8_e4m3fn_x4
+E5 = mybir.dt.float8_e5m2_x4
+E2 = mybir.dt.float4_e2m1fn_x4
+ALU = mybir.AluOpType
+ACT = mybir.ActivationFunctionType
+
+P = 128
+PACK = 4
+HALF = 128
+PAD = 4
+
+
+def tile_list_sum_pickgaps_stepped_overtable_rowpeaks_kernel(
+    tc, xf, fk, w_words, w_scales, so, fl, w2_words, w2_scales, tb, wb_words, wb_scales, rs, offs, offs2, offs3, out
+):
+    nc = tc.nc
+    halves = range(J // HALF)
+    with ExitStack() as ctx:
+        sb = ctx.enter_context(tc.tile_pool(name="sb", bufs=1))
+        ps = ctx.enter_context(tc.psum_pool(name="ps", bufs=1))
+
+        def tile(name, shape, dtype):
+            return sb.tile(shape, dtype, name=name, align_bytes=64)
+
+        list1 = tile("list1", [P, J // 16], U16)
+        list2 = tile("list2", [P, J // 16], U16)
+        list3 = tile("list3", [P, J // 16], U16)
+        xf_sb = [tile("xf%d" % t, [P, T], F32) for t in range(PACK)]
+        tb_sb = [tile("tb%d" % a, [P, 2, V], F32) for a in range(2)]
+        so_sb = tile("so_sb", [P, PACK, J], F32)
+        fk_sb = tile("fk_sb", [P, PACK], F32)
+        fl_sb = tile("fl_sb", [P, PACK], F32)
+        w_raw = tile("w_raw", [P, R], U32)
+        w2_raw = tile("w2_raw", [P, R], U32)
+        ws_raw = tile("ws_raw", [P, R], U8)
+        wb_sb = tile("wb_sb", [P, 2 * N], U8)
+        wbs_sb = tile("wbs_sb", [P, N], U8)
+        rs_sb = tile("rs_sb", [P, J // HALF, N], F32)
+
+        nc.vector.memset(ws_raw[:].bitcast(I32), 0)
+        nc.vector.memset(wbs_sb[:].bitcast(I32), 0)
+        scaled = tile("scaled", [P, PACK, PAD + J], F32)
+
+        xf_v = xf.rearrange("(p t) c -> p t c", t=PACK)
+        tb_v = tb.rearrange("(p t) c -> p t c", t=PACK)
+
+        def words(ap):
+            return ap[0].rearrange("p c b -> p (c b)").bitcast(I32)
+
+        def load_scale_rows(eng, dst, first, src, q):
+            eng.dma_start(
+                out=dst[32 * q + first : 32 * q + first + 4, :].bitcast(I32),
+                in_=src[0, 4 * q : 4 * q + 4, :].bitcast(I32),
+            )
+
+        nc.sync.dma_start(list2[:], offs2)
+        nc.scalar.dma_start(out=xf_sb[0][:], in_=xf_v[:, 0, :])
+        nc.sync.dma_start(list1[:], offs)
+        for t in range(1, PACK):
+            nc.sync.dma_start(out=xf_sb[t][:], in_=xf_v[:, t, :])
+        nc.gpsimd.dma_start(out=fk_sb[:], in_=fk.rearrange("(p t) o -> p (t o)", t=PACK))
+        nc.gpsimd.dma_start(out=fl_sb[:], in_=fl.rearrange("(p t) o -> p (t o)", t=PACK))
+        nc.sync.dma_start(out=so_sb[:], in_=so.rearrange("(p t) c -> p t c", t=PACK))
+        for q in range(4):
+            load_scale_rows(nc.sync, ws_raw, 4, w_scales, q)
+        nc.sync.dma_start(out=w_raw[:].bitcast(I32), in_=words(w_words))
+        for q in range(2):
+            load_scale_rows(nc.sync, ws_raw, 0, w2_scales, q)
+        nc.sync.dma_start(out=w2_raw[:].bitcast(I32), in_=words(w2_words))
+        for q in range(2, 4):
+            load_scale_rows(nc.sync, ws_raw, 0, w2_scales, q)
+        nc.sync.dma_start(out=tb_sb[0][:], in_=tb_v[:, 0:2, :])
+        nc.sync.dma_start(list3[:], offs3)
+        nc.sync.dma_start(out=tb_sb[1][:], in_=tb_v[:, 2:4, :])
+        nc.sync.dma_start(out=wb_sb[:].bitcast(I32), in_=wb_words[0].bitcast(I32))
+        nc.sync.dma_start(out=rs_sb[:], in_=rs.rearrange("(h p) n -> p h n", p=P))
+        for q in range(4):
+            load_scale_rows(nc.gpsimd, wbs_sb, 0, wb_scales, q)
+
+        before_first = scaled[:, :, PAD - 1 : PAD].bitcast(U32)
+        nc.scalar.activation(before_first, before_first, ACT.Copy, scale=0.0)
+        second = tile("second", [P, PACK, J], F32)
+        gap = tile("gap", [P, PACK, J], F32)
+        for t in range(PACK):
+            nc.scalar.activation(second[:, t, :], xf_sb[t][:].indirect(list2[:]), ACT.Copy)
+            nc.vector.tensor_tensor(gap[:, t, :], xf_sb[t][:].indirect(list1[:]), second[:, t, :], ALU.subtract)
+
+        def weave_out(ap):
+            return ap.rearrange("p (c i) t -> p c t i", i=4)
+
+        def weave_in(ap):
+            return ap.rearrange("p t (c i) -> p c t i", i=4)
+
+        u_bf = [tile("u_bf%d" % h, [P, HALF, PACK], BF16) for h in halves]
+        u2_bf = [tile("u2_bf%d" % h, [P, HALF, PACK], BF16) for h in halves]
+        hid_bf = [tile("hid_bf%d" % h, [P, HALF, PACK], BF16) for h in halves]
+        codes = {}
+        planes = {}
+        for nm in ("u", "u2", "hid"):
+            for h in halves:
+                codes[nm, h] = tile("%s_codes%d" % (nm, h), [P, HALF], U32)
+                planes[nm, h] = tile("%s_plane%d" % (nm, h), [P, HALF], U8)
+
+        def quantize(nm, h, src, fmt):
+            nc.vector.quantize_mx(
+                out=codes[nm, h][:].bitcast(fmt), scales=planes[nm, h][:], in_=src[:].rearrange("p j t -> p (j t)")
+            )
+
+        fk_b = fk_sb[:].unsqueeze(1).unsqueeze(3).to_broadcast([P, HALF // 4, PACK, 4])
+        for h in halves:
+            cols = slice(h * HALF, (h + 1) * HALF)
+            nc.vector.tensor_tensor(weave_out(u_bf[h][:]), weave_in(gap[:, :, cols]), fk_b, ALU.mult)
+        for t in range(PACK):
+            nc.scalar.activation(scaled[:, t, PAD:], so_sb[:, t, :], ACT.Copy, scale=fl_sb[:, t : t + 1])
+        for h in halves:
+            quantize("u", h, u_bf[h], E4)
+
+        w_sb = tile("w_sb", [P, PACK, P], U32)
+        w2_sb = tile("w2_sb", [P, PACK, P], U32)
+        ws_sb = tile("ws_sb", [P, PACK, P], U8)
+        for dst, src in ((w_sb, w_raw), (w2_sb, w2_raw)):
+            nc.scalar.copy(weave_in(dst[:]), src[:].rearrange("p (c i t) -> p c t i", i=4, t=PACK))
+        nc.vector.tensor_copy(ws_sb[:], ws_raw[:].rearrange("p (q t) -> p t q", t=PACK))
+
+        for h in halves:
+            lo = PAD + h * HALF
+            nc.vector.scalar_tensor_tensor(
+                out=u2_bf[h][:],
+                in0=scaled[:, :, lo - 1 : lo - 1 + HALF].rearrange("p t j -> p j t"),
+                scalar=-0.8,
+                in1=scaled[:, :, lo : lo + HALF].rearrange("p t j -> p j t"),
+                op0=ALU.mult,
+                op1=ALU.add,
+            )
+        for h in halves:
+            quantize("u2", h, u2_bf[h], E4)
+
+        picked = tile("picked", [P, PACK, J], F32)
+        for t in range(PACK):
+            nc.scalar.activation(picked[:, t, :], tb_sb[t // 2][:, t % 2, :].indirect(list3[:]), ACT.Copy)
+
+        acc = [ps.tile([P, PACK, HALF], F32, name="acc%d" % h) for h in halves]
+        for h in halves:
+            for t in range(PACK):
+                nc.tensor.matmul_mx(
+                    out=acc[h][:, t, :],
+                    lhsT=w_sb[:, t, :].bitcast(E4),
+                    lhsT_scale=ws_sb[4:, t, :],
+                    rhs=codes["u", h][:].bitcast(E4),
+                    rhs_scale=planes["u", h][:],
+                    start=(t == 0),
+                    stop=False,
+                )
+        for h in halves:
+            for t in range(PACK):
+                nc.tensor.matmul_mx(
+                    out=acc[h][:, t, :],
+                    lhsT=w2_sb[:, t, :].bitcast(E5),
+                    lhsT_scale=ws_sb[:, t, :],
+                    rhs=codes["u2", h][:].bitcast(E4),
+                    rhs_scale=planes["u2", h][:],
+                    start=False,
+                    stop=(t == PACK - 1),
+                )
+
+        rs3 = tile("rs3", [P, J // HALF, N], F32)
+        nc.scalar.mul(rs3[:], rs_sb[:], 0.3)
+
+        over = [tile("over%d" % h, [P, PACK, HALF], F32) for h in halves]
+        prod = [ps.tile([P, N], F32, name="prod%d" % h) for h in halves]
+        mag = [tile("mag%d" % h, [P, N], F32) for h in halves]
+        peak = [tile("peak%d" % h, [P, 1], F32) for h in halves]
+        inv = [tile("inv%d" % h, [P, 1], F32) for h in halves]
+        res = [tile("res%d" % h, [P, N], F32) for h in halves]
+        for h in halves:
+            cols = slice(h * HALF, (h + 1) * HALF)
+            nc.vector.tensor_tensor(over[h][:], acc[h][:], picked[:, :, cols], ALU.subtract)
+            nc.scalar.activation(weave_out(hid_bf[h][:]), weave_in(over[h][:]), ACT.Relu)
+        for h in halves:
+            quantize("hid", h, hid_bf[h], E5)
+            nc.tensor.matmul_mx(
+                out=prod[h][:],
+                lhsT=codes["hid", h][:].bitcast(E5),
+                lhsT_scale=planes["hid", h][:],
+                rhs=wb_sb[:].bitcast(E2),
+                rhs_scale=wbs_sb[:],
+                start=True,
+                stop=True,
+            )
+            nc.scalar.activation(mag[h][:], prod[h][:], ACT.Abs)
+        for h in halves:
+            nc.vector.tensor_scalar(mag[h][:], mag[h][:], 0.2, None, ALU.add, ALU.max, accum_out=peak[h][:])
+            nc.vector.reciprocal(inv[h][:], peak[h][:])
+            nc.vector.scalar_tensor_tensor(
+                out=res[h][:], in0=prod[h][:], scalar=inv[h][:], in1=rs3[:, h, :], op0=ALU.mult, op1=ALU.add
+            )
+            nc.sync.dma_start(out=out[h * HALF : (h + 1) * HALF, :], in_=res[h][:])

@@ -32,8 +32,8 @@ def tile_list_sum_pickgaps_stepped_overtable_rowpeaks_kernel(
         sb = ctx.enter_context(tc.tile_pool(name="sb", bufs=1))
         ps = ctx.enter_context(tc.psum_pool(name="ps", bufs=1))
 
-        def tile(name, shape, dtype):
-            return sb.tile(shape, dtype, name=name, align_bytes=64)
+        def tile(name, shape, dtype, tag=None):
+            return sb.tile(shape, dtype, name=name, tag=tag or name, align_bytes=64)
 
         list1 = tile("list1", [P, J // 16], U16)
         list2 = tile("list2", [P, J // 16], U16)
@@ -50,7 +50,7 @@ def tile_list_sum_pickgaps_stepped_overtable_rowpeaks_kernel(
         wbs_sb = tile("wbs_sb", [P, N], U8)
         rs_sb = tile("rs_sb", [P, J // HALF, N], F32)
 
-        nc.vector.memset(ws_raw[:].bitcast(I32), 0)
+        nc.gpsimd.memset(ws_raw[:].bitcast(I32), 0)
         nc.vector.memset(wbs_sb[:].bitcast(I32), 0)
         scaled = tile("scaled", [P, PACK, PAD + J], F32)
 
@@ -69,26 +69,31 @@ def tile_list_sum_pickgaps_stepped_overtable_rowpeaks_kernel(
         nc.sync.dma_start(list2[:], offs2)
         nc.scalar.dma_start(out=xf_sb[0][:], in_=xf_v[:, 0, :])
         nc.sync.dma_start(list1[:], offs)
-        for t in range(1, PACK):
-            nc.sync.dma_start(out=xf_sb[t][:], in_=xf_v[:, t, :])
+        nc.sync.dma_start(out=xf_sb[1][:], in_=xf_v[:, 1, :])
+        nc.sync.dma_start(out=xf_sb[2][:], in_=xf_v[:, 2, :])
+        nc.sync.dma_start(out=xf_sb[3][:], in_=xf_v[:, 3, :])
+        nc.sync.dma_start(out=so_sb[:], in_=so.rearrange("(p t) c -> p t c", t=PACK))
+        nc.sync.dma_start(out=w_raw[:].bitcast(I32), in_=words(w_words))
         nc.gpsimd.dma_start(out=fk_sb[:], in_=fk.rearrange("(p t) o -> p (t o)", t=PACK))
         nc.gpsimd.dma_start(out=fl_sb[:], in_=fl.rearrange("(p t) o -> p (t o)", t=PACK))
-        nc.sync.dma_start(out=so_sb[:], in_=so.rearrange("(p t) c -> p t c", t=PACK))
-        for q in range(4):
-            load_scale_rows(nc.sync, ws_raw, 4, w_scales, q)
-        nc.sync.dma_start(out=w_raw[:].bitcast(I32), in_=words(w_words))
-        for q in range(2):
-            load_scale_rows(nc.sync, ws_raw, 0, w2_scales, q)
-        nc.sync.dma_start(out=w2_raw[:].bitcast(I32), in_=words(w2_words))
-        for q in range(2, 4):
-            load_scale_rows(nc.sync, ws_raw, 0, w2_scales, q)
-        nc.sync.dma_start(out=tb_sb[0][:], in_=tb_v[:, 0:2, :])
+        load_scale_rows(nc.sync, ws_raw, 4, w_scales, 0)
+        load_scale_rows(nc.sync, ws_raw, 4, w_scales, 1)
+        load_scale_rows(nc.sync, ws_raw, 4, w_scales, 2)
         nc.sync.dma_start(list3[:], offs3)
+        nc.sync.dma_start(out=w2_raw[:].bitcast(I32), in_=words(w2_words))
+        nc.sync.dma_start(out=tb_sb[0][:], in_=tb_v[:, 0:2, :])
+        load_scale_rows(nc.sync, ws_raw, 4, w_scales, 3)
+        load_scale_rows(nc.sync, ws_raw, 0, w2_scales, 0)
+        load_scale_rows(nc.sync, ws_raw, 0, w2_scales, 1)
+        load_scale_rows(nc.sync, ws_raw, 0, w2_scales, 2)
+        load_scale_rows(nc.sync, ws_raw, 0, w2_scales, 3)
         nc.sync.dma_start(out=tb_sb[1][:], in_=tb_v[:, 2:4, :])
         nc.sync.dma_start(out=wb_sb[:].bitcast(I32), in_=wb_words[0].bitcast(I32))
         nc.sync.dma_start(out=rs_sb[:], in_=rs.rearrange("(h p) n -> p h n", p=P))
-        for q in range(4):
-            load_scale_rows(nc.gpsimd, wbs_sb, 0, wb_scales, q)
+        load_scale_rows(nc.gpsimd, wbs_sb, 0, wb_scales, 0)
+        load_scale_rows(nc.gpsimd, wbs_sb, 0, wb_scales, 1)
+        load_scale_rows(nc.gpsimd, wbs_sb, 0, wb_scales, 2)
+        load_scale_rows(nc.gpsimd, wbs_sb, 0, wb_scales, 3)
 
         before_first = scaled[:, :, PAD - 1 : PAD].bitcast(U32)
         nc.scalar.activation(before_first, before_first, ACT.Copy, scale=0.0)
@@ -105,7 +110,6 @@ def tile_list_sum_pickgaps_stepped_overtable_rowpeaks_kernel(
             return ap.rearrange("p t (c i) -> p c t i", i=4)
 
         u_bf = [tile("u_bf%d" % h, [P, HALF, PACK], BF16) for h in halves]
-        u2_bf = [tile("u2_bf%d" % h, [P, HALF, PACK], BF16) for h in halves]
         hid_bf = [tile("hid_bf%d" % h, [P, HALF, PACK], BF16) for h in halves]
         codes = {}
         planes = {}
@@ -133,24 +137,31 @@ def tile_list_sum_pickgaps_stepped_overtable_rowpeaks_kernel(
         ws_sb = tile("ws_sb", [P, PACK, P], U8)
         for dst, src in ((w_sb, w_raw), (w2_sb, w2_raw)):
             nc.scalar.copy(weave_in(dst[:]), src[:].rearrange("p (c i t) -> p c t i", i=4, t=PACK))
-        nc.vector.tensor_copy(ws_sb[:], ws_raw[:].rearrange("p (q t) -> p t q", t=PACK))
 
-        for h in halves:
+        def stepped(h, dst):
             lo = PAD + h * HALF
             nc.vector.scalar_tensor_tensor(
-                out=u2_bf[h][:],
+                out=dst[:],
                 in0=scaled[:, :, lo - 1 : lo - 1 + HALF].rearrange("p t j -> p j t"),
                 scalar=-0.8,
                 in1=scaled[:, :, lo : lo + HALF].rearrange("p t j -> p j t"),
                 op0=ALU.mult,
                 op1=ALU.add,
             )
-        for h in halves:
-            quantize("u2", h, u2_bf[h], E4)
 
-        picked = tile("picked", [P, PACK, J], F32)
-        for t in range(PACK):
-            nc.scalar.activation(picked[:, t, :], tb_sb[t // 2][:, t % 2, :].indirect(list3[:]), ACT.Copy)
+        u2_bf0 = tile("u2_bf0", [P, HALF, PACK], BF16)
+        stepped(0, u2_bf0)
+        nc.vector.tensor_copy(ws_sb[:], ws_raw[:].rearrange("p (q t) -> p t q", t=PACK))
+        quantize("u2", 0, u2_bf0, E4)
+        u2_bf1 = tile("u2_bf1", [P, HALF, PACK], BF16, tag="ws_raw")
+        stepped(1, u2_bf1)
+        quantize("u2", 1, u2_bf1, E4)
+
+        picked = [tile("picked%d" % h, [P, PACK, HALF], F32) for h in halves]
+        for h in halves:
+            entries = list3[:, h * HALF // 16 : (h + 1) * HALF // 16]
+            for t in range(PACK):
+                nc.scalar.activation(picked[h][:, t, :], tb_sb[t // 2][:, t % 2, :].indirect(entries), ACT.Copy)
 
         acc = [ps.tile([P, PACK, HALF], F32, name="acc%d" % h) for h in halves]
         for h in halves:
@@ -164,7 +175,6 @@ def tile_list_sum_pickgaps_stepped_overtable_rowpeaks_kernel(
                     start=(t == 0),
                     stop=False,
                 )
-        for h in halves:
             for t in range(PACK):
                 nc.tensor.matmul_mx(
                     out=acc[h][:, t, :],
@@ -176,8 +186,6 @@ def tile_list_sum_pickgaps_stepped_overtable_rowpeaks_kernel(
                     stop=(t == PACK - 1),
                 )
 
-        rs3 = tile("rs3", [P, J // HALF, N], F32)
-        nc.scalar.mul(rs3[:], rs_sb[:], 0.3)
 
         over = [tile("over%d" % h, [P, PACK, HALF], F32) for h in halves]
         prod = [ps.tile([P, N], F32, name="prod%d" % h) for h in halves]
@@ -187,8 +195,11 @@ def tile_list_sum_pickgaps_stepped_overtable_rowpeaks_kernel(
         res = [tile("res%d" % h, [P, N], F32) for h in halves]
         for h in halves:
             cols = slice(h * HALF, (h + 1) * HALF)
-            nc.vector.tensor_tensor(over[h][:], acc[h][:], picked[:, :, cols], ALU.subtract)
+            nc.vector.tensor_tensor(over[h][:], acc[h][:], picked[h][:], ALU.subtract)
             nc.scalar.activation(weave_out(hid_bf[h][:]), weave_in(over[h][:]), ACT.Relu)
+        rs3 = [tile("rs3_%d" % h, [P, N], F32, tag="over%d" % h) for h in halves]
+        for h in halves:
+            nc.scalar.mul(rs3[h][:], rs_sb[:, h, :], 0.3)
         for h in halves:
             quantize("hid", h, hid_bf[h], E5)
             nc.tensor.matmul_mx(
@@ -205,6 +216,6 @@ def tile_list_sum_pickgaps_stepped_overtable_rowpeaks_kernel(
             nc.vector.tensor_scalar(mag[h][:], mag[h][:], 0.2, None, ALU.add, ALU.max, accum_out=peak[h][:])
             nc.vector.reciprocal(inv[h][:], peak[h][:])
             nc.vector.scalar_tensor_tensor(
-                out=res[h][:], in0=prod[h][:], scalar=inv[h][:], in1=rs3[:, h, :], op0=ALU.mult, op1=ALU.add
+                out=res[h][:], in0=prod[h][:], scalar=inv[h][:], in1=rs3[h][:], op0=ALU.mult, op1=ALU.add
             )
-            nc.sync.dma_start(out=out[h * HALF : (h + 1) * HALF, :], in_=res[h][:])
+            (nc.sync, nc.scalar)[h].dma_start(out=out[h * HALF : (h + 1) * HALF, :], in_=res[h][:])

from contextlib import ExitStack

import concourse.mybir as mybir

K, T, J, R, F, V, N = 512, 512, 256, 512, 512, 512, 256
FLOPS = 2 * J * (K * R + F * R + R * N)

F32 = mybir.dt.float32
BF16 = mybir.dt.bfloat16
I32 = mybir.dt.int32
U32 = mybir.dt.uint32
U16 = mybir.dt.uint16
U8 = mybir.dt.uint8
E4 = mybir.dt.float8_e4m3fn_x4
E5 = mybir.dt.float8_e5m2_x4
E2 = mybir.dt.float4_e2m1fn_x4
ALU = mybir.AluOpType
ACT = mybir.ActivationFunctionType

P = 128
PACK = 4
HALF = 128
PAD = 4


def tile_list_sum_pickgaps_stepped_overtable_rowpeaks_kernel(
    tc, xf, fk, w_words, w_scales, so, fl, w2_words, w2_scales, tb, wb_words, wb_scales, rs, offs, offs2, offs3, out
):
    nc = tc.nc
    halves = range(J // HALF)
    with ExitStack() as ctx:
        sb = ctx.enter_context(tc.tile_pool(name="sb", bufs=1))
        ps = ctx.enter_context(tc.psum_pool(name="ps", bufs=1))

        def tile(name, shape, dtype, tag=None):
            return sb.tile(shape, dtype, name=name, tag=tag or name, align_bytes=64)

        list1 = tile("list1", [P, J // 16], U16)
        list2 = tile("list2", [P, J // 16], U16)
        list3 = tile("list3", [P, J // 16], U16)
        xf_sb = [tile("xf%d" % t, [P, T], F32) for t in range(PACK)]
        tb_sb = [tile("tb%d" % a, [P, 2, V], F32) for a in range(2)]
        so_sb = tile("so_sb", [P, PACK, J], F32)
        fk_sb = tile("fk_sb", [P, PACK], F32)
        fl_sb = tile("fl_sb", [P, PACK], F32)
        w_raw = tile("w_raw", [P, R], U32)
        w2_raw = tile("w2_raw", [P, R], U32)
        ws_raw = tile("ws_raw", [P, R], U8)
        wb_sb = tile("wb_sb", [P, 2 * N], U8)
        wbs_sb = tile("wbs_sb", [P, N], U8)
        rs_sb = tile("rs_sb", [P, J // HALF, N], F32)

        nc.gpsimd.memset(ws_raw[:].bitcast(I32), 0)
        nc.vector.memset(wbs_sb[:].bitcast(I32), 0)
        scaled = tile("scaled", [P, PACK, PAD + J], F32)

        xf_v = xf.rearrange("(p t) c -> p t c", t=PACK)
        tb_v = tb.rearrange("(p t) c -> p t c", t=PACK)

        def words(ap):
            return ap[0].rearrange("p c b -> p (c b)").bitcast(I32)

        def load_scale_rows(eng, dst, first, src, q):
            eng.dma_start(
                out=dst[32 * q + first : 32 * q + first + 4, :].bitcast(I32),
                in_=src[0, 4 * q : 4 * q + 4, :].bitcast(I32),
            )

        nc.sync.dma_start(list2[:], offs2)
        nc.scalar.dma_start(out=xf_sb[0][:], in_=xf_v[:, 0, :])
        nc.sync.dma_start(list1[:], offs)
        nc.sync.dma_start(out=xf_sb[1][:], in_=xf_v[:, 1, :])
        nc.sync.dma_start(out=xf_sb[2][:], in_=xf_v[:, 2, :])
        nc.sync.dma_start(out=xf_sb[3][:], in_=xf_v[:, 3, :])
        nc.sync.dma_start(out=so_sb[:], in_=so.rearrange("(p t) c -> p t c", t=PACK))
        nc.sync.dma_start(out=w_raw[:].bitcast(I32), in_=words(w_words))
        nc.gpsimd.dma_start(out=fk_sb[:], in_=fk.rearrange("(p t) o -> p (t o)", t=PACK))
        nc.gpsimd.dma_start(out=fl_sb[:], in_=fl.rearrange("(p t) o -> p (t o)", t=PACK))
        load_scale_rows(nc.sync, ws_raw, 4, w_scales, 0)
        load_scale_rows(nc.sync, ws_raw, 4, w_scales, 1)
        load_scale_rows(nc.sync, ws_raw, 4, w_scales, 2)
        nc.sync.dma_start(list3[:], offs3)
        nc.sync.dma_start(out=w2_raw[:].bitcast(I32), in_=words(w2_words))
        nc.sync.dma_start(out=tb_sb[0][:], in_=tb_v[:, 0:2, :])
        load_scale_rows(nc.sync, ws_raw, 4, w_scales, 3)
        load_scale_rows(nc.sync, ws_raw, 0, w2_scales, 0)
        load_scale_rows(nc.sync, ws_raw, 0, w2_scales, 1)
        load_scale_rows(nc.sync, ws_raw, 0, w2_scales, 2)
        load_scale_rows(nc.sync, ws_raw, 0, w2_scales, 3)
        nc.sync.dma_start(out=tb_sb[1][:], in_=tb_v[:, 2:4, :])
        nc.sync.dma_start(out=wb_sb[:].bitcast(I32), in_=wb_words[0].bitcast(I32))
        nc.sync.dma_start(out=rs_sb[:], in_=rs.rearrange("(h p) n -> p h n", p=P))
        load_scale_rows(nc.gpsimd, wbs_sb, 0, wb_scales, 0)
        load_scale_rows(nc.gpsimd, wbs_sb, 0, wb_scales, 1)
        load_scale_rows(nc.gpsimd, wbs_sb, 0, wb_scales, 2)
        load_scale_rows(nc.gpsimd, wbs_sb, 0, wb_scales, 3)

        before_first = scaled[:, :, PAD - 1 : PAD].bitcast(U32)
        nc.scalar.activation(before_first, before_first, ACT.Copy, scale=0.0)
        second = tile("second", [P, PACK, J], F32)
        gap = tile("gap", [P, PACK, J], F32)
        for t in range(PACK):
            nc.scalar.activation(second[:, t, :], xf_sb[t][:].indirect(list2[:]), ACT.Copy)
            nc.vector.tensor_tensor(gap[:, t, :], xf_sb[t][:].indirect(list1[:]), second[:, t, :], ALU.subtract)

        def weave_out(ap):
            return ap.rearrange("p (c i) t -> p c t i", i=4)

        def weave_in(ap):
            return ap.rearrange("p t (c i) -> p c t i", i=4)

        u_bf = [tile("u_bf%d" % h, [P, HALF, PACK], BF16) for h in halves]
        hid_bf = [tile("hid_bf%d" % h, [P, HALF, PACK], BF16) for h in halves]
        codes = {}
        planes = {}
        for nm in ("u", "u2", "hid"):
            for h in halves:
                codes[nm, h] = tile("%s_codes%d" % (nm, h), [P, HALF], U32)
                planes[nm, h] = tile("%s_plane%d" % (nm, h), [P, HALF], U8)

        def quantize(nm, h, src, fmt):
            nc.vector.quantize_mx(
                out=codes[nm, h][:].bitcast(fmt), scales=planes[nm, h][:], in_=src[:].rearrange("p j t -> p (j t)")
            )

        fk_b = fk_sb[:].unsqueeze(1).unsqueeze(3).to_broadcast([P, HALF // 4, PACK, 4])
        for h in halves:
            cols = slice(h * HALF, (h + 1) * HALF)
            nc.vector.tensor_tensor(weave_out(u_bf[h][:]), weave_in(gap[:, :, cols]), fk_b, ALU.mult)
        for t in range(PACK):
            nc.scalar.activation(scaled[:, t, PAD:], so_sb[:, t, :], ACT.Copy, scale=fl_sb[:, t : t + 1])
        for h in halves:
            quantize("u", h, u_bf[h], E4)

        w_sb = tile("w_sb", [P, PACK, P], U32)
        w2_sb = tile("w2_sb", [P, PACK, P], U32)
        ws_sb = tile("ws_sb", [P, PACK, P], U8)
        for dst, src in ((w_sb, w_raw), (w2_sb, w2_raw)):
            nc.scalar.copy(weave_in(dst[:]), src[:].rearrange("p (c i t) -> p c t i", i=4, t=PACK))

        def stepped(h, dst):
            lo = PAD + h * HALF
            nc.vector.scalar_tensor_tensor(
                out=dst[:],
                in0=scaled[:, :, lo - 1 : lo - 1 + HALF].rearrange("p t j -> p j t"),
                scalar=-0.8,
                in1=scaled[:, :, lo : lo + HALF].rearrange("p t j -> p j t"),
                op0=ALU.mult,
                op1=ALU.add,
            )

        u2_bf0 = tile("u2_bf0", [P, HALF, PACK], BF16)
        stepped(0, u2_bf0)
        nc.vector.tensor_copy(ws_sb[:], ws_raw[:].rearrange("p (q t) -> p t q", t=PACK))
        quantize("u2", 0, u2_bf0, E4)
        u2_bf1 = tile("u2_bf1", [P, HALF, PACK], BF16, tag="ws_raw")
        stepped(1, u2_bf1)
        quantize("u2", 1, u2_bf1, E4)

        picked = [tile("picked%d" % h, [P, PACK, HALF], F32) for h in halves]
        for h in halves:
            entries = list3[:, h * HALF // 16 : (h + 1) * HALF // 16]
            for t in range(PACK):
                nc.scalar.activation(picked[h][:, t, :], tb_sb[t // 2][:, t % 2, :].indirect(entries), ACT.Copy)

        acc = [ps.tile([P, PACK, HALF], F32, name="acc%d" % h) for h in halves]
        for h in halves:
            for t in range(PACK):
                nc.tensor.matmul_mx(
                    out=acc[h][:, t, :],
                    lhsT=w_sb[:, t, :].bitcast(E4),
                    lhsT_scale=ws_sb[4:, t, :],
                    rhs=codes["u", h][:].bitcast(E4),
                    rhs_scale=planes["u", h][:],
                    start=(t == 0),
                    stop=False,
                )
            for t in range(PACK):
                nc.tensor.matmul_mx(
                    out=acc[h][:, t, :],
                    lhsT=w2_sb[:, t, :].bitcast(E5),
                    lhsT_scale=ws_sb[:, t, :],
                    rhs=codes["u2", h][:].bitcast(E4),
                    rhs_scale=planes["u2", h][:],
                    start=False,
                    stop=(t == PACK - 1),
                )


        over = [tile("over%d" % h, [P, PACK, HALF], F32) for h in halves]
        prod = [ps.tile([P, N], F32, name="prod%d" % h) for h in halves]
        mag = [tile("mag%d" % h, [P, N], F32) for h in halves]
        peak = [tile("peak%d" % h, [P, 1], F32) for h in halves]
        inv = [tile("inv%d" % h, [P, 1], F32) for h in halves]
        res = [tile("res%d" % h, [P, N], F32) for h in halves]
        for h in halves:
            cols = slice(h * HALF, (h + 1) * HALF)
            nc.vector.tensor_tensor(over[h][:], acc[h][:], picked[h][:], ALU.subtract)
            nc.scalar.activation(weave_out(hid_bf[h][:]), weave_in(over[h][:]), ACT.Relu)
        rs3 = [tile("rs3_%d" % h, [P, N], F32, tag="over%d" % h) for h in halves]
        for h in halves:
            nc.scalar.mul(rs3[h][:], rs_sb[:, h, :], 0.3)
        for h in halves:
            quantize("hid", h, hid_bf[h], E5)
            nc.tensor.matmul_mx(
                out=prod[h][:],
                lhsT=codes["hid", h][:].bitcast(E5),
                lhsT_scale=planes["hid", h][:],
                rhs=wb_sb[:].bitcast(E2),
                rhs_scale=wbs_sb[:],
                start=True,
                stop=True,
            )
            nc.scalar.activation(mag[h][:], prod[h][:], ACT.Abs)
        for h in halves:
            nc.vector.tensor_scalar(mag[h][:], mag[h][:], 0.2, None, ALU.add, ALU.max, accum_out=peak[h][:])
            nc.vector.reciprocal(inv[h][:], peak[h][:])
            nc.vector.scalar_tensor_tensor(
                out=res[h][:], in0=prod[h][:], scalar=inv[h][:], in1=rs3[h][:], op0=ALU.mult, op1=ALU.add
            )
            (nc.sync, nc.scalar)[h].dma_start(out=out[h * HALF : (h + 1) * HALF, :], in_=res[h][:])
